import numpy as np
import ml_dtypes


def mxq(x, axis, fmt="e4m3"):
    dtype, down = {"e4m3": (ml_dtypes.float8_e4m3fn, 7), "e5m2": (ml_dtypes.float8_e5m2, 14)}[fmt]
    v = np.moveaxis(np.asarray(x, np.float32).astype(ml_dtypes.bfloat16).astype(np.float64), axis, -1)
    blocks = v.reshape(v.shape[:-1] + (-1, 32))
    amax = np.abs(blocks).max(-1, keepdims=True)
    byte = np.maximum(np.where(amax > 0, np.frexp(amax)[1] - 1 + 127, 0) - down, 1)
    scale = np.exp2(byte - 127.0)
    codes = (blocks / scale).astype(np.float32).astype(dtype).astype(np.float64)
    return np.moveaxis((codes * scale).reshape(v.shape), -1, axis)


WIDE = False


def mx_kscale(k):
    if not WIDE:
        return np.ones(k)
    levels = np.array([10, -10, 5, -5, 0])
    if k % 512:
        return np.exp2(np.random.permutation(np.resize(levels, k // 32))).repeat(32)
    a = np.empty((k // 512, 16))
    for p in range(k // 512):
        a[p, :8] = np.random.permutation(np.resize(levels, 8))
        for g in range(8):
            far = levels[np.abs(levels - a[p, g]) >= 10]
            a[p, g + 8] = far[np.random.randint(len(far))]
    return np.exp2(a.ravel()).repeat(32)


BF16 = ml_dtypes.bfloat16


def bf(x):
    return np.asarray(x, np.float32).astype(BF16)


def f64(x):
    return np.asarray(x).astype(np.float64)


E2M1 = np.array([0.0, 0.5, 1.0, 1.5, 2.0, 3.0, 4.0, 6.0, -0.0, -0.5, -1.0, -1.5, -2.0, -3.0, -4.0, -6.0])


def pack_weight(w, fmt):
    k, n = w.shape
    w = f64(bf(w)).reshape(k // 32, 32, n)
    amax = np.abs(w).max(1)
    if fmt == "e4m3":
        byte = np.frexp(amax)[1] - 1 + 127 - 7
    else:
        mant, ex = np.frexp(amax / 6.0)
        byte = np.where(mant > 0.5, ex, ex - 1) + 127
    byte = np.clip(np.where(amax > 0, byte, 1), 1, 254)
    scaled = (w * np.exp2(127.0 - byte)[:, None, :]).reshape(k, n).astype(np.float32)
    by_word = np.ascontiguousarray(scaled.reshape(k // 512, 128, 4, n).transpose(0, 1, 3, 2))
    if fmt == "e4m3":
        words = by_word.astype(ml_dtypes.float8_e4m3fn).view(np.uint8)
    else:
        c = by_word.astype(ml_dtypes.float4_e2m1fn).view(np.uint8) & 0xF
        words = c[..., 0::2] | (c[..., 1::2] << 4)
    return np.ascontiguousarray(words), np.ascontiguousarray(byte.astype(np.uint8).reshape(k // 512, 16, n))


def unpack_weight(words, scales, fmt):
    g, p, n, _ = words.shape
    if fmt == "e4m3":
        vals = np.ascontiguousarray(words).view(ml_dtypes.float8_e4m3fn).astype(np.float64)
    else:
        nib = np.empty((g, p, n, 4), np.uint8)
        nib[..., 0::2] = words & 0xF
        nib[..., 1::2] = words >> 4
        vals = E2M1[nib]
    vals = vals * np.repeat(np.exp2(scales.astype(np.float64) - 127.0), 8, axis=1)[..., None]
    return vals.transpose(0, 1, 3, 2).reshape(g * 512, n)
def pack4(w):
    words, scales = pack_weight(w, "e2m1")
    return words.reshape(words.shape[0], 128, -1), scales


def unpack4(words, scales):
    return unpack_weight(words.reshape(words.shape[0], 128, -1, 2), scales, "e2m1")


U, L, T = 512, 1024, 2048


def setup_inputs():
    s, r, c = mx_kscale(L), mx_kscale(L), mx_kscale(T)
    a = np.random.standard_normal((L, U))
    v = np.random.standard_normal((L, T))
    f = v.T + 0.5 * np.random.standard_normal((T, L))
    b = a + 0.5 * np.random.standard_normal((L, U))
    a_words, a_scales = pack4(a * s[:, None])
    v_words, v_scales = pack4(v / np.sqrt(L) / T ** 0.3 / s[:, None] * c)
    return {"a_words": a_words, "a_scales": a_scales,
            "v_words": v_words, "v_scales": v_scales,
            "f": bf(f / c[:, None] * r),
            "b": bf(b / np.sqrt(L) / T ** 0.3 / r[:, None])}


def reference(a_words, a_scales, v_words, v_scales, f, b):
    h = unpack4(a_words, a_scales).T @ unpack4(v_words, v_scales)
    z = mxq(f64(f), 1, "e4m3") @ mxq(f64(b), 0, "e4m3")
    e = mxq(h, 1, "e4m3") @ mxq(z, 0, "e4m3")
    power = e * e
    total = power.sum(axis=1)
    leak = total - np.diagonal(power)
    rate = np.log(total / leak)
    return rate, e

@@ -1,0 +1,386 @@
+from contextlib import ExitStack
+
+import concourse.mybir as mybir
+from concourse.masks import make_identity
+
+F32 = mybir.dt.float32
+BF16 = mybir.dt.bfloat16
+I32 = mybir.dt.int32
+U32 = mybir.dt.uint32
+U8 = mybir.dt.uint8
+FP8X4 = mybir.dt.float8_e4m3fn_x4
+FP4X4 = mybir.dt.float4_e2m1fn_x4
+ALU = mybir.AluOpType
+ACT = mybir.ActivationFunctionType
+
+P = 128
+USERS, PATHS, ANT = 512, 1024, 2048
+PASSES = 2
+GROUPS = 4
+FLOPS = 2 * USERS * PATHS * ANT * 2 + 2 * USERS * USERS * ANT
+WARM = 7
+
+
+def tile_downlink_leakage_rate_s12_kernel(tc, a_words, a_scales, v_words, v_scales, f, b, out_0, out_1):
+    nc = tc.nc
+    with ExitStack() as ctx:
+        keep = ctx.enter_context(tc.tile_pool(name="keep", bufs=1))
+        per = ctx.enter_context(tc.tile_pool(name="per", bufs=4))
+        rows = ctx.enter_context(tc.tile_pool(name="rows", bufs=16))
+        psum = ctx.enter_context(tc.psum_pool(name="psum", bufs=8))
+        ctx.enter_context(tc.manual_schedule())
+
+        aw = keep.tile([P, PASSES, 1024], U8, name="aw", align_bytes=64)
+        asc = keep.tile([P, PASSES, 512], U8, name="asc", align_bytes=64)
+        vs_raw = keep.tile([P, PASSES, 2048], U8, name="vs_raw", align_bytes=64)
+        vs = keep.tile([P, PASSES, 4, 512], U8, name="vs", align_bytes=64)
+        zero = keep.tile([P, 512], BF16, name="zero")
+        ident = keep.tile([P, P], F32, name="ident")
+        perm = keep.tile([P, 4, 4, 8], F32, name="perm")
+        rate = keep.tile([P, P], F32, name="rate")
+        ln_warm = keep.tile([P, 1], F32, name="ln_warm")
+        part_a = keep.tile([P, 4], F32, name="part_a")
+        part_b = keep.tile([P, 4], F32, name="part_b")
+        part_off = keep.tile([P, 4], F32, name="part_off")
+        signal = keep.tile([P, 4], F32, name="signal")
+        leak = keep.tile([P, 4], F32, name="leak")
+        inv = keep.tile([P, 4], F32, name="inv")
+        rate_rows = keep.tile([4, P], F32, name="rate_rows")
+        b_codes = keep.tile([P, PASSES, 512], U32, name="b_codes", align_bytes=64)
+        b_scales = keep.tile([P, PASSES, 512], U8, name="b_scales", align_bytes=64)
+        b_raw = []
+        b_grp = []
+        for g in range(PASSES):
+            br = keep.tile([P, 4, 512], BF16, name=f"br{g}", align_bytes=64)
+            bg = keep.tile([P, 512, 4], BF16, name=f"bg{g}", align_bytes=64)
+            b_raw.append(br)
+            b_grp.append(bg)
+        v_raw = []
+        v_cod = []
+        f_raw = []
+        f_grp = []
+        f_cod = []
+        f_scl = []
+        h_grp = []
+        h_cod = []
+        h_scl = []
+        z_grp = []
+        z_cod = []
+        z_scl = []
+        for G in range(GROUPS):
+            vr = per.tile([P, PASSES, 1024], U8, name="vr", align_bytes=64)
+            vc = per.tile([P, 4, PASSES, 256], U8, name="vc", align_bytes=64)
+            fg = per.tile([P, PASSES, 4, P, 4], BF16, name="fg", align_bytes=64)
+            fc = per.tile([P, PASSES, 4, P], U32, name="fc", align_bytes=64)
+            fs = per.tile([P, PASSES, 4, P], U8, name="fs", align_bytes=64)
+            hg = per.tile([P, 512, 4], BF16, name="hg", align_bytes=64)
+            hc = per.tile([P, 512], U32, name="hc", align_bytes=64)
+            hs = per.tile([P, 512], U8, name="hs", align_bytes=64)
+            zg = per.tile([P, 512, 4], BF16, name="zg", align_bytes=64)
+            zc = per.tile([P, 512], U32, name="zc", align_bytes=64)
+            zs = per.tile([P, 512], U8, name="zs", align_bytes=64)
+            v_raw.append(vr)
+            v_cod.append(vc)
+            f_grp.append(fg)
+            f_cod.append(fc)
+            f_scl.append(fs)
+            h_grp.append(hg)
+            h_cod.append(hc)
+            h_scl.append(hs)
+            z_grp.append(zg)
+            z_cod.append(zc)
+            z_scl.append(zs)
+            f_raw.append([])
+            for r in range(4):
+                fr = rows.tile([P, 1024], BF16, name="fr", align_bytes=64)
+                f_raw[G].append(fr)
+
+        v_view = v_words.rearrange("g p c -> p g c")
+
+        def load_v(G):
+            nc.sync.dma_start(out=v_raw[G][:].bitcast(I32), in_=v_view[:, :, 1024 * G : 1024 * (G + 1)].bitcast(I32))
+
+        def load_f(G):
+            for r in range(4):
+                n0 = 512 * G + 128 * r
+                nc.sync.dma_start(out=f_raw[G][r][:], in_=f[n0 : n0 + 128, :])
+
+        def load_b(g):
+            nc.sync.dma_start(out=b_raw[g][:], in_=b[512 * g : 512 * (g + 1), :].rearrange("(p j) w -> p j w", j=4))
+
+        def permute_v(G):
+            src = v_raw[G][:].rearrange("p g c -> p (g c)").bitcast(I32)
+            dst = v_cod[G][:].rearrange("p t g c -> p (t g c)").bitcast(I32)
+            nc.vector.tensor_copy(
+                out=dst.rearrange("p (t b w) -> p t b w", t=4, w=4),
+                in_=src.rearrange("p (b t w) -> p t b w", t=4, w=4),
+            )
+
+        def permute_v_scales(g):
+            src = vs_raw[:, g, :].bitcast(I32)
+            dst = vs[:, g, :, :].rearrange("p t c -> p (t c)").bitcast(I32)
+            nc.vector.tensor_copy(
+                out=dst.rearrange("p (t b w) -> p t b w", t=4, w=2),
+                in_=src.rearrange("p (b t w) -> p t b w", t=4, w=2),
+            )
+
+        def interleave_b(g):
+            nc.vector.tensor_copy(out=b_grp[g][:], in_=b_raw[g][:].rearrange("p j w -> p w j"))
+
+        def quant(codes, scales, grouped):
+            nc.vector.quantize_mx(out=codes.bitcast(FP8X4), scales=scales, in_=grouped)
+
+        def quant_b(g):
+            quant(b_codes[:, g, :], b_scales[:, g, :], b_grp[g][:].rearrange("p w j -> p (w j)"))
+
+        def quant_f(G, g):
+            quant(
+                f_cod[G][:, g].rearrange("p t m -> p (t m)"),
+                f_scl[G][:, g].rearrange("p t m -> p (t m)"),
+                f_grp[G][:, g].rearrange("p t m j -> p (t m j)"),
+            )
+
+        def quant_cols(cod, scl, grp, lo, hi):
+            quant(cod[:, lo:hi], scl[:, lo:hi], grp[:, lo:hi, :].rearrange("p n j -> p (n j)"))
+
+        def copy(on_vector, out, in_):
+            if on_vector:
+                nc.vector.tensor_copy(out=out, in_=in_)
+            else:
+                nc.scalar.copy(out, in_)
+
+        def turn_f(G, r, on_vector):
+            bank = psum.tile([P, 2, PASSES, P], F32, name="bank")
+            words = f_raw[G][r][:].bitcast(F32)
+            for g in range(PASSES):
+                for u in range(2):
+                    nc.tensor.transpose(
+                        bank[:, u, g, :],
+                        words[:, 256 * g + u : 256 * (g + 1) : 2],
+                        perm[:].rearrange("p t b i -> p (t b i)"),
+                    )
+            dst = f_grp[G][:].rearrange("p g t m j -> p (g t) (m j)").bitcast(F32)
+            copy(
+                on_vector,
+                dst[:, :, 64 * r : 64 * (r + 1)].rearrange("p q (c u) -> p q c u", u=2),
+                bank[:].rearrange("p u g c -> p u (g c)").rearrange("p u (q c) -> p q c u", c=32),
+            )
+
+        def channel(G, n, on_vector):
+            bank = psum.tile([P, 4, P], F32, name="bank")
+            for t in range(4):
+                for g in range(PASSES):
+                    nc.tensor.matmul_mx(
+                        out=bank[:, t, :],
+                        lhsT=v_cod[G][:, t, g, :].bitcast(FP4X4),
+                        lhsT_scale=vs[:, g, t, 128 * G : 128 * (G + 1)],
+                        rhs=aw[:, g, 256 * n : 256 * (n + 1)].bitcast(FP4X4),
+                        rhs_scale=asc[:, g, 128 * n : 128 * (n + 1)],
+                        start=(g == 0),
+                        stop=(g == PASSES - 1),
+                    )
+            copy(on_vector, h_grp[G][:, 128 * n : 128 * (n + 1), :], bank[:].rearrange("p t c -> p c t"))
+
+        def precode(G, n, on_vector):
+            bank = psum.tile([P, 4, P], F32, name="bank")
+            for t in range(4):
+                for g in range(PASSES):
+                    nc.tensor.matmul_mx(
+                        out=bank[:, t, :],
+                        lhsT=f_cod[G][:, g, t, :].bitcast(FP8X4),
+                        lhsT_scale=f_scl[G][:, g, t, :],
+                        rhs=b_codes[:, g, 128 * n : 128 * (n + 1)].bitcast(FP8X4),
+                        rhs_scale=b_scales[:, g, 128 * n : 128 * (n + 1)],
+                        start=(g == 0),
+                        stop=(g == PASSES - 1),
+                    )
+            copy(on_vector, z_grp[G][:, 128 * n : 128 * (n + 1), :], bank[:].rearrange("p t c -> p c t"))
+
+        def quant_h(G):
+            quant_cols(h_cod[G], h_scl[G], h_grp[G], 0, 512)
+
+        def quant_z(G, lo, hi):
+            quant_cols(z_cod[G], z_scl[G], z_grp[G], lo, hi)
+
+        e_banks = {}
+
+        def effective(m, G):
+            if G == 0:
+                eb = psum.tile([P, 512], F32, name="bank")
+                e_banks[m] = eb
+            nc.tensor.matmul_mx(
+                out=e_banks[m][:],
+                lhsT=h_cod[G][:, 128 * m : 128 * (m + 1)].bitcast(FP8X4),
+                lhsT_scale=h_scl[G][:, 128 * m : 128 * (m + 1)],
+                rhs=z_cod[G][:].bitcast(FP8X4),
+                rhs_scale=z_scl[G][:],
+                start=(G == 0),
+                stop=(G == GROUPS - 1),
+            )
+
+        e_rows = {}
+        diag = {}
+        off = {}
+
+        def finish_tiles(m):
+            dg = per.tile([P, P], F32, name="dg")
+            of = per.tile([P, P], F32, name="of")
+            es = per.tile([P, 512], F32, name="es")
+            diag[m] = dg
+            off[m] = of
+            e_rows[m] = es
+
+        def store_rows(m):
+            nc.vector.tensor_copy(out=e_rows[m][:], in_=e_banks[m][:])
+            nc.sync.dma_start(out=out_1[128 * m : 128 * (m + 1), :], in_=e_rows[m][:])
+
+        def split_diag(m, eng, src):
+            lo, hi = 128 * m, 128 * (m + 1)
+            eng.tensor_tensor(out=diag[m][:], in0=src[:, lo:hi], in1=ident[:], op=ALU.mult)
+            eng.tensor_tensor(out=off[m][:], in0=src[:, lo:hi], in1=diag[m][:], op=ALU.subtract)
+
+        def square_rest(m, src):
+            lo, hi = 128 * m, 128 * (m + 1)
+            sq = per.tile([P, 512], F32, name="sq")
+            if lo > 0:
+                nc.scalar.activation(sq[:, 0:lo], src[:, 0:lo], ACT.Square, accum_out=part_a[:, m : m + 1])
+            if hi < 512:
+                nc.scalar.activation(sq[:, hi:512], src[:, hi:512], ACT.Square, accum_out=part_b[:, m : m + 1])
+
+        def square_block(m):
+            nc.scalar.activation(diag[m][:], diag[m][:], ACT.Square, accum_out=signal[:, m : m + 1])
+            nc.scalar.activation(off[m][:], off[m][:], ACT.Square, accum_out=part_off[:, m : m + 1])
+
+        def log_rate(m):
+            nc.scalar.activation(rate[:, m : m + 1], inv[:, m : m + 1], ACT.Ln, bias=1.0, scale=signal[:, m : m + 1])
+
+        nc.gpsimd.memset(asc[:].rearrange("p g c -> p (g c)").bitcast(I32), 0)
+        nc.vector.memset(vs_raw[:].rearrange("p g c -> p (g c)").bitcast(I32), 0)
+        nc.vector.memset(zero[:], 0.0)
+        nc.vector.memset(ln_warm[:], 1.0)
+        nc.scalar.activation(ln_warm[:], ln_warm[:], ACT.Ln)
+        nc.sync.dma_start(out=aw[:].bitcast(I32), in_=a_words.rearrange("g p c -> p g c").bitcast(I32))
+        load_v(0)
+        for Q in range(4):
+            nc.sync.dma_start(
+                out=vs_raw[32 * Q : 32 * Q + 4, :, :].bitcast(I32),
+                in_=v_scales[:, 4 * Q : 4 * Q + 4, :].rearrange("g r n -> r g n").bitcast(I32),
+            )
+        for Q in range(4):
+            eng = nc.sync if Q < 2 else nc.gpsimd
+            eng.dma_start(
+                out=asc[32 * Q : 32 * Q + 4, :, :].bitcast(I32),
+                in_=a_scales[:, 4 * Q : 4 * Q + 4, :].rearrange("g r n -> r g n").bitcast(I32),
+            )
+        load_v(1)
+        load_b(0)
+        load_b(1)
+        load_f(0)
+        load_v(2)
+        load_f(1)
+        load_v(3)
+        load_f(2)
+        load_f(3)
+
+        make_identity(nc, ident[:])
+        nc.gpsimd.memset(rate[:], 0.0)
+        nc.gpsimd.memset(part_a[:], 0.0)
+        nc.gpsimd.memset(part_b[:], 0.0)
+        warm_bank = psum.tile([P, 512], F32, name="bank")
+        for i in range(WARM):
+            nc.tensor.matmul(out=warm_bank[:], lhsT=zero[:, 0:128], rhs=zero[:], start=True, stop=True)
+
+        permute_v_scales(0)
+        permute_v_scales(1)
+        permute_v(0)
+        for n in range(4):
+            channel(0, n, False)
+        permute_v(1)
+        nc.vector.tensor_copy(out=perm[:], in_=ident[:].rearrange("p (b t i) -> p t b i", b=4, t=4))
+        interleave_b(0)
+        for n in range(4):
+            channel(1, n, False)
+        interleave_b(1)
+        quant_h(0)
+        quant_b(0)
+        quant_b(1)
+        for r in range(4):
+            turn_f(0, r, r % 2 == 1)
+        quant_h(1)
+        permute_v(2)
+        for n in range(4):
+            channel(2, n, False)
+        quant_f(0, 0)
+        quant_f(0, 1)
+        for r in range(4):
+            turn_f(1, r, r % 2 == 1)
+        quant_h(2)
+        quant_f(1, 0)
+        permute_v(3)
+        for n in range(4):
+            precode(0, n, n % 2 == 1)
+        quant_f(1, 1)
+        for n in range(4):
+            channel(3, n, False)
+        quant_z(0, 0, 512)
+        for r in range(4):
+            turn_f(2, r, r % 2 == 1)
+        quant_h(3)
+        for n in range(4):
+            if n == 1:
+                quant_f(2, 0)
+            if n == 3:
+                quant_f(2, 1)
+            precode(1, n, n % 2 == 1)
+        for r in range(4):
+            turn_f(3, r, r % 2 == 1)
+        quant_z(1, 0, 512)
+        for n in range(4):
+            if n == 1:
+                quant_f(3, 0)
+            if n == 3:
+                quant_f(3, 1)
+            precode(2, n, n % 2 == 1)
+        for n in range(4):
+            precode(3, n, n % 2 == 1)
+            if n == 1:
+                quant_z(2, 0, 512)
+        for m in range(4):
+            finish_tiles(m)
+        for m in range(2):
+            for G in range(3):
+                effective(m, G)
+        quant_z(3, 0, 256)
+        quant_z(3, 256, 384)
+        quant_z(3, 384, 512)
+        effective(0, 3)
+        effective(1, 3)
+        for m in range(2):
+            store_rows(m)
+            split_diag(m, nc.gpsimd, e_rows[m])
+            square_rest(m, e_rows[m])
+            square_block(m)
+        for G in range(4):
+            effective(2, G)
+        store_rows(2)
+        split_diag(2, nc.gpsimd, e_rows[2])
+        square_rest(2, e_rows[2])
+        for G in range(4):
+            effective(3, G)
+        square_rest(3, e_banks[3])
+        square_block(2)
+        split_diag(3, nc.vector, e_banks[3])
+        store_rows(3)
+        square_block(3)
+        nc.gpsimd.tensor_tensor(out=leak[:, 0:3], in0=part_a[:, 0:3], in1=part_b[:, 0:3], op=ALU.add)
+        nc.gpsimd.tensor_tensor(out=leak[:, 0:3], in0=leak[:, 0:3], in1=part_off[:, 0:3], op=ALU.add)
+        nc.vector.reciprocal(inv[:, 0:3], leak[:, 0:3])
+        nc.vector.tensor_tensor(out=leak[:, 3:4], in0=part_a[:, 3:4], in1=part_off[:, 3:4], op=ALU.add)
+        nc.vector.reciprocal(inv[:, 3:4], leak[:, 3:4])
+        for m in range(4):
+            log_rate(m)
+
+        last = psum.tile([P, 4, P], F32, name="bank")
+        nc.tensor.transpose(last[:, 0, :], rate[:], ident[:])
+        nc.vector.tensor_copy(out=rate_rows[:], in_=last[0:4, 0, :])
+        nc.sync.dma_start(out=out_0.rearrange("(m p) -> m p", p=P), in_=rate_rows[:])

@@ -116,13 +116,10 @@ def tile_downlink_leakage_rate_s12_kernel(tc, a_words, a_scales, v_words, v_scal
                 in_=src.rearrange("p (b t w) -> p t b w", t=4, w=4),
             )
 
-        def permute_v_scales(g):
-            src = vs_raw[:, g, :].bitcast(I32)
-            dst = vs[:, g, :, :].rearrange("p t c -> p (t c)").bitcast(I32)
-            nc.vector.tensor_copy(
-                out=dst.rearrange("p (t b w) -> p t b w", t=4, w=2),
-                in_=src.rearrange("p (b t w) -> p t b w", t=4, w=2),
-            )
+        def permute_v_scales(g, lo, hi):
+            src = vs_raw[:, g, :].bitcast(I32).rearrange("p (b t w) -> p t b w", t=4, w=2)
+            dst = vs[:, g, :, :].rearrange("p t c -> p (t c)").bitcast(I32).rearrange("p (t b w) -> p t b w", t=4, w=2)
+            nc.vector.tensor_copy(out=dst[:, :, lo:hi, :], in_=src[:, :, lo:hi, :])
 
         def interleave_b(g):
             nc.vector.tensor_copy(out=b_grp[g][:], in_=b_raw[g][:].rearrange("p j w -> p w j"))
@@ -149,16 +146,23 @@ def tile_downlink_leakage_rate_s12_kernel(tc, a_words, a_scales, v_words, v_scal
             else:
                 nc.scalar.copy(out, in_)
 
+        f_even_odd = {}
+
+        def sort_f(G, r):
+            fe = rows.tile([P, PASSES, 2, P], F32, name="fe", bufs=8, align_bytes=64)
+            f_even_odd[G, r] = fe
+            nc.vector.tensor_copy(out=fe[:], in_=f_raw[G][r][:].bitcast(F32).rearrange("p (g x u) -> p g u x", g=PASSES, u=2))
+
         def turn_f(G, r, on_vector):
             bank = psum.tile([P, 2, PASSES, P], F32, name="bank")
             words = f_raw[G][r][:].bitcast(F32)
             for g in range(PASSES):
                 for u in range(2):
-                    nc.tensor.transpose(
-                        bank[:, u, g, :],
-                        words[:, 256 * g + u : 256 * (g + 1) : 2],
-                        perm[:].rearrange("p t b i -> p (t b i)"),
-                    )
+                    if (G, r) in f_even_odd:
+                        src = f_even_odd[G, r][:, g, u, :]
+                    else:
+                        src = words[:, 256 * g + u : 256 * (g + 1) : 2]
+                    nc.tensor.transpose(bank[:, u, g, :], src, perm[:].rearrange("p t b i -> p (t b i)"))
             dst = f_grp[G][:].rearrange("p g t m j -> p (g t) (m j)").bitcast(F32)
             copy(
                 on_vector,
@@ -247,19 +251,24 @@ def tile_downlink_leakage_rate_s12_kernel(tc, a_words, a_scales, v_words, v_scal
             if hi < 512:
                 nc.scalar.activation(sq[:, hi:512], src[:, hi:512], ACT.Square, accum_out=part_b[:, m : m + 1])
 
-        def square_block(m):
-            nc.scalar.activation(diag[m][:], diag[m][:], ACT.Square, accum_out=signal[:, m : m + 1])
+        def signal_power(m):
+            junk = per.tile([P, P], F32, name="junk")
+            nc.vector.scalar_tensor_tensor(
+                out=junk[:], in0=diag[m][:], scalar=1.0, in1=diag[m][:], op0=ALU.mult, op1=ALU.mult, accum_out=signal[:, m : m + 1]
+            )
+
+        def square_off(m):
             nc.scalar.activation(off[m][:], off[m][:], ACT.Square, accum_out=part_off[:, m : m + 1])
 
         def log_rate(m):
             nc.scalar.activation(rate[:, m : m + 1], inv[:, m : m + 1], ACT.Ln, bias=1.0, scale=signal[:, m : m + 1])
 
+        nc.gpsimd.dma_start(out=aw[:].bitcast(I32), in_=a_words.rearrange("g p c -> p g c").bitcast(I32))
         nc.gpsimd.memset(asc[:].rearrange("p g c -> p (g c)").bitcast(I32), 0)
         nc.vector.memset(vs_raw[:].rearrange("p g c -> p (g c)").bitcast(I32), 0)
         nc.vector.memset(zero[:], 0.0)
         nc.vector.memset(ln_warm[:], 1.0)
         nc.scalar.activation(ln_warm[:], ln_warm[:], ACT.Ln)
-        nc.sync.dma_start(out=aw[:].bitcast(I32), in_=a_words.rearrange("g p c -> p g c").bitcast(I32))
         load_v(0)
         for Q in range(4):
             nc.sync.dma_start(
@@ -267,7 +276,7 @@ def tile_downlink_leakage_rate_s12_kernel(tc, a_words, a_scales, v_words, v_scal
                 in_=v_scales[:, 4 * Q : 4 * Q + 4, :].rearrange("g r n -> r g n").bitcast(I32),
             )
         for Q in range(4):
-            eng = nc.sync if Q < 2 else nc.gpsimd
+            eng = nc.sync if Q < 3 else nc.gpsimd
             eng.dma_start(
                 out=asc[32 * Q : 32 * Q + 4, :, :].bitcast(I32),
                 in_=a_scales[:, 4 * Q : 4 * Q + 4, :].rearrange("g r n -> r g n").bitcast(I32),
@@ -290,59 +299,65 @@ def tile_downlink_leakage_rate_s12_kernel(tc, a_words, a_scales, v_words, v_scal
         for i in range(WARM):
             nc.tensor.matmul(out=warm_bank[:], lhsT=zero[:, 0:128], rhs=zero[:], start=True, stop=True)
 
-        permute_v_scales(0)
-        permute_v_scales(1)
         permute_v(0)
+        permute_v_scales(0, 0, 16)
+        permute_v_scales(1, 0, 16)
         for n in range(4):
             channel(0, n, False)
         permute_v(1)
+        permute_v_scales(0, 16, 64)
+        permute_v_scales(1, 16, 64)
         nc.vector.tensor_copy(out=perm[:], in_=ident[:].rearrange("p (b t i) -> p t b i", b=4, t=4))
-        interleave_b(0)
         for n in range(4):
             channel(1, n, False)
+        interleave_b(0)
         interleave_b(1)
         quant_h(0)
+        permute_v(2)
+        for r in range(4):
+            turn_f(0, r, r == 3)
         quant_b(0)
         quant_b(1)
-        for r in range(4):
-            turn_f(0, r, r % 2 == 1)
         quant_h(1)
-        permute_v(2)
         for n in range(4):
             channel(2, n, False)
         quant_f(0, 0)
         quant_f(0, 1)
-        for r in range(4):
-            turn_f(1, r, r % 2 == 1)
-        quant_h(2)
-        quant_f(1, 0)
         permute_v(3)
+        for r in range(4):
+            turn_f(1, r, r == 3)
+        quant_h(2)
+        for r in range(2):
+            sort_f(2, r)
         for n in range(4):
-            precode(0, n, n % 2 == 1)
+            precode(0, n, n == 3)
+        quant_f(1, 0)
         quant_f(1, 1)
+        for r in range(2, 4):
+            sort_f(2, r)
         for n in range(4):
             channel(3, n, False)
+        for r in range(4):
+            turn_f(2, r, r == 3)
         quant_z(0, 0, 512)
         for r in range(4):
-            turn_f(2, r, r % 2 == 1)
-        quant_h(3)
+            sort_f(3, r)
         for n in range(4):
             if n == 1:
                 quant_f(2, 0)
-            if n == 3:
                 quant_f(2, 1)
-            precode(1, n, n % 2 == 1)
+            precode(1, n, n == 3)
+        quant_h(3)
         for r in range(4):
-            turn_f(3, r, r % 2 == 1)
-        quant_z(1, 0, 512)
+            turn_f(3, r, r == 3)
         for n in range(4):
             if n == 1:
                 quant_f(3, 0)
-            if n == 3:
                 quant_f(3, 1)
-            precode(2, n, n % 2 == 1)
+            precode(2, n, n == 3)
+        quant_z(1, 0, 512)
         for n in range(4):
-            precode(3, n, n % 2 == 1)
+            precode(3, n, n == 3)
             if n == 1:
                 quant_z(2, 0, 512)
         for m in range(4):
@@ -355,23 +370,24 @@ def tile_downlink_leakage_rate_s12_kernel(tc, a_words, a_scales, v_words, v_scal
         quant_z(3, 384, 512)
         effective(0, 3)
         effective(1, 3)
-        for m in range(2):
+        for G in range(4):
+            effective(2, G)
+        for G in range(4):
+            effective(3, G)
+        for m in range(3):
             store_rows(m)
             split_diag(m, nc.gpsimd, e_rows[m])
             square_rest(m, e_rows[m])
-            square_block(m)
-        for G in range(4):
-            effective(2, G)
-        store_rows(2)
-        split_diag(2, nc.gpsimd, e_rows[2])
-        square_rest(2, e_rows[2])
-        for G in range(4):
-            effective(3, G)
+            if m > 0:
+                signal_power(m - 1)
+                square_off(m - 1)
         square_rest(3, e_banks[3])
-        square_block(2)
         split_diag(3, nc.vector, e_banks[3])
         store_rows(3)
-        square_block(3)
+        square_off(2)
+        signal_power(2)
+        nc.scalar.activation(diag[3][:], diag[3][:], ACT.Square, accum_out=signal[:, 3:4])
+        square_off(3)
         nc.gpsimd.tensor_tensor(out=leak[:, 0:3], in0=part_a[:, 0:3], in1=part_b[:, 0:3], op=ALU.add)
         nc.gpsimd.tensor_tensor(out=leak[:, 0:3], in0=leak[:, 0:3], in1=part_off[:, 0:3], op=ALU.add)
         nc.vector.reciprocal(inv[:, 0:3], leak[:, 0:3])

@@ -18,7 +18,7 @@ USERS, PATHS, ANT = 512, 1024, 2048
 PASSES = 2
 GROUPS = 4
 FLOPS = 2 * USERS * PATHS * ANT * 2 + 2 * USERS * USERS * ANT
-WARM = 7
+WARM = 11
 
 
 def tile_downlink_leakage_rate_s12_kernel(tc, a_words, a_scales, v_words, v_scales, f, b, out_0, out_1):
@@ -149,7 +149,7 @@ def tile_downlink_leakage_rate_s12_kernel(tc, a_words, a_scales, v_words, v_scal
         f_even_odd = {}
 
         def sort_f(G, r):
-            fe = rows.tile([P, PASSES, 2, P], F32, name="fe", bufs=8, align_bytes=64)
+            fe = rows.tile([P, PASSES, 2, P], F32, name="fe", bufs=12, align_bytes=64)
             f_even_odd[G, r] = fe
             nc.vector.tensor_copy(out=fe[:], in_=f_raw[G][r][:].bitcast(F32).rearrange("p (g x u) -> p g u x", g=PASSES, u=2))
 
@@ -222,6 +222,23 @@ def tile_downlink_leakage_rate_s12_kernel(tc, a_words, a_scales, v_words, v_scal
                 stop=(G == GROUPS - 1),
             )
 
+        e_halves = {}
+
+        def effective_half(half, G):
+            if G == 0:
+                eb = psum.tile([P, 256], F32, name="bank")
+                e_halves[half] = eb
+            cols = slice(256 * half, 256 * (half + 1))
+            nc.tensor.matmul_mx(
+                out=e_halves[half][:],
+                lhsT=h_cod[G][:, 384:512].bitcast(FP8X4),
+                lhsT_scale=h_scl[G][:, 384:512],
+                rhs=z_cod[G][:, cols].bitcast(FP8X4),
+                rhs_scale=z_scl[G][:, cols],
+                start=(G == 0),
+                stop=(G == GROUPS - 1),
+            )
+
         e_rows = {}
         diag = {}
         off = {}
@@ -263,12 +280,12 @@ def tile_downlink_leakage_rate_s12_kernel(tc, a_words, a_scales, v_words, v_scal
         def log_rate(m):
             nc.scalar.activation(rate[:, m : m + 1], inv[:, m : m + 1], ACT.Ln, bias=1.0, scale=signal[:, m : m + 1])
 
-        nc.gpsimd.dma_start(out=aw[:].bitcast(I32), in_=a_words.rearrange("g p c -> p g c").bitcast(I32))
         nc.gpsimd.memset(asc[:].rearrange("p g c -> p (g c)").bitcast(I32), 0)
         nc.vector.memset(vs_raw[:].rearrange("p g c -> p (g c)").bitcast(I32), 0)
         nc.vector.memset(zero[:], 0.0)
         nc.vector.memset(ln_warm[:], 1.0)
         nc.scalar.activation(ln_warm[:], ln_warm[:], ACT.Ln)
+        nc.sync.dma_start(out=aw[:].bitcast(I32), in_=a_words.rearrange("g p c -> p g c").bitcast(I32))
         load_v(0)
         for Q in range(4):
             nc.sync.dma_start(
@@ -276,18 +293,17 @@ def tile_downlink_leakage_rate_s12_kernel(tc, a_words, a_scales, v_words, v_scal
                 in_=v_scales[:, 4 * Q : 4 * Q + 4, :].rearrange("g r n -> r g n").bitcast(I32),
             )
         for Q in range(4):
-            eng = nc.sync if Q < 3 else nc.gpsimd
-            eng.dma_start(
+            nc.sync.dma_start(
                 out=asc[32 * Q : 32 * Q + 4, :, :].bitcast(I32),
                 in_=a_scales[:, 4 * Q : 4 * Q + 4, :].rearrange("g r n -> r g n").bitcast(I32),
             )
         load_v(1)
         load_b(0)
+        load_v(2)
         load_b(1)
         load_f(0)
-        load_v(2)
-        load_f(1)
         load_v(3)
+        load_f(1)
         load_f(2)
         load_f(3)
 
@@ -311,53 +327,55 @@ def tile_downlink_leakage_rate_s12_kernel(tc, a_words, a_scales, v_words, v_scal
         for n in range(4):
             channel(1, n, False)
         interleave_b(0)
-        interleave_b(1)
-        quant_h(0)
         permute_v(2)
-        for r in range(4):
-            turn_f(0, r, r == 3)
-        quant_b(0)
-        quant_b(1)
-        quant_h(1)
+        interleave_b(1)
         for n in range(4):
             channel(2, n, False)
-        quant_f(0, 0)
-        quant_f(0, 1)
+        quant_b(0)
+        quant_b(1)
+        for r in range(4):
+            sort_f(0, r)
         permute_v(3)
         for r in range(4):
-            turn_f(1, r, r == 3)
-        quant_h(2)
-        for r in range(2):
-            sort_f(2, r)
-        for n in range(4):
-            precode(0, n, n == 3)
-        quant_f(1, 0)
-        quant_f(1, 1)
-        for r in range(2, 4):
-            sort_f(2, r)
+            turn_f(0, r, False)
+        quant_h(0)
+        for r in range(4):
+            sort_f(1, r)
         for n in range(4):
             channel(3, n, False)
         for r in range(4):
-            turn_f(2, r, r == 3)
-        quant_z(0, 0, 512)
-        for r in range(4):
+            sort_f(2, r)
+        quant_f(0, 0)
+        quant_f(0, 1)
+        for r in range(2):
             sort_f(3, r)
-        for n in range(4):
-            if n == 1:
-                quant_f(2, 0)
-                quant_f(2, 1)
-            precode(1, n, n == 3)
-        quant_h(3)
         for r in range(4):
-            turn_f(3, r, r == 3)
+            turn_f(1, r, r % 2 == 1)
+        for r in range(2, 4):
+            sort_f(3, r)
+        for r in range(4):
+            turn_f(2, r, r % 2 == 1)
+        quant_f(1, 0)
+        quant_f(1, 1)
+        for r in range(4):
+            turn_f(3, r, r % 2 == 1)
+        quant_f(2, 0)
+        quant_f(2, 1)
         for n in range(4):
-            if n == 1:
-                quant_f(3, 0)
-                quant_f(3, 1)
+            precode(0, n, False)
+        quant_f(3, 0)
+        quant_f(3, 1)
+        quant_h(1)
+        quant_h(2)
+        for n in range(4):
+            precode(1, n, n == 3)
+        quant_z(0, 0, 512)
+        quant_h(3)
+        for n in range(4):
             precode(2, n, n == 3)
         quant_z(1, 0, 512)
         for n in range(4):
-            precode(3, n, n == 3)
+            precode(3, n, n % 2 == 1)
             if n == 1:
                 quant_z(2, 0, 512)
         for m in range(4):
@@ -372,8 +390,9 @@ def tile_downlink_leakage_rate_s12_kernel(tc, a_words, a_scales, v_words, v_scal
         effective(1, 3)
         for G in range(4):
             effective(2, G)
-        for G in range(4):
-            effective(3, G)
+        for half in (1, 0):
+            for G in range(4):
+                effective_half(half, G)
         for m in range(3):
             store_rows(m)
             split_diag(m, nc.gpsimd, e_rows[m])
@@ -381,18 +400,27 @@ def tile_downlink_leakage_rate_s12_kernel(tc, a_words, a_scales, v_words, v_scal
             if m > 0:
                 signal_power(m - 1)
                 square_off(m - 1)
-        square_rest(3, e_banks[3])
-        split_diag(3, nc.vector, e_banks[3])
-        store_rows(3)
-        square_off(2)
+        hi_bank, lo_bank = e_halves[1], e_halves[0]
+        nc.vector.tensor_tensor(out=diag[3][:], in0=hi_bank[:, 128:256], in1=ident[:], op=ALU.mult)
         signal_power(2)
+        nc.vector.tensor_tensor(out=off[3][:], in0=hi_bank[:, 128:256], in1=diag[3][:], op=ALU.subtract)
+        square_off(2)
+        sq3 = per.tile([P, 512], F32, name="sq")
+        nc.scalar.activation(sq3[:, 256:384], hi_bank[:, 0:128], ACT.Square, accum_out=part_b[:, 3:4])
+        nc.vector.tensor_copy(out=e_rows[3][:, 256:512], in_=hi_bank[:])
+        nc.sync.dma_start(out=out_1[384:512, 256:512], in_=e_rows[3][:, 256:512])
         nc.scalar.activation(diag[3][:], diag[3][:], ACT.Square, accum_out=signal[:, 3:4])
         square_off(3)
+        nc.scalar.activation(sq3[:, 0:256], lo_bank[:], ACT.Square, accum_out=part_a[:, 3:4])
         nc.gpsimd.tensor_tensor(out=leak[:, 0:3], in0=part_a[:, 0:3], in1=part_b[:, 0:3], op=ALU.add)
         nc.gpsimd.tensor_tensor(out=leak[:, 0:3], in0=leak[:, 0:3], in1=part_off[:, 0:3], op=ALU.add)
         nc.vector.reciprocal(inv[:, 0:3], leak[:, 0:3])
-        nc.vector.tensor_tensor(out=leak[:, 3:4], in0=part_a[:, 3:4], in1=part_off[:, 3:4], op=ALU.add)
+        nc.vector.scalar_tensor_tensor(
+            out=leak[:, 3:4], in0=part_a[:, 3:4], scalar=part_b[:, 3:4], in1=part_off[:, 3:4], op0=ALU.add, op1=ALU.add
+        )
         nc.vector.reciprocal(inv[:, 3:4], leak[:, 3:4])
+        nc.vector.tensor_copy(out=e_rows[3][:, 0:256], in_=lo_bank[:])
+        nc.sync.dma_start(out=out_1[384:512, 0:256], in_=e_rows[3][:, 0:256])
         for m in range(4):
             log_rate(m)
 

@@ -18,7 +18,7 @@ USERS, PATHS, ANT = 512, 1024, 2048
 PASSES = 2
 GROUPS = 4
 FLOPS = 2 * USERS * PATHS * ANT * 2 + 2 * USERS * USERS * ANT
-WARM = 11
+WARM = 13
 
 
 def tile_downlink_leakage_rate_s12_kernel(tc, a_words, a_scales, v_words, v_scales, f, b, out_0, out_1):
@@ -26,7 +26,7 @@ def tile_downlink_leakage_rate_s12_kernel(tc, a_words, a_scales, v_words, v_scal
     with ExitStack() as ctx:
         keep = ctx.enter_context(tc.tile_pool(name="keep", bufs=1))
         per = ctx.enter_context(tc.tile_pool(name="per", bufs=4))
-        rows = ctx.enter_context(tc.tile_pool(name="rows", bufs=16))
+        rows = ctx.enter_context(tc.tile_pool(name="rows", bufs=8))
         psum = ctx.enter_context(tc.psum_pool(name="psum", bufs=8))
         ctx.enter_context(tc.manual_schedule())
 
@@ -39,9 +39,8 @@ def tile_downlink_leakage_rate_s12_kernel(tc, a_words, a_scales, v_words, v_scal
         perm = keep.tile([P, 4, 4, 8], F32, name="perm")
         rate = keep.tile([P, P], F32, name="rate")
         ln_warm = keep.tile([P, 1], F32, name="ln_warm")
-        part_a = keep.tile([P, 4], F32, name="part_a")
-        part_b = keep.tile([P, 4], F32, name="part_b")
-        part_off = keep.tile([P, 4], F32, name="part_off")
+        total = keep.tile([P, 4], F32, name="total")
+        half_sum = keep.tile([P, 2], F32, name="half_sum")
         signal = keep.tile([P, 4], F32, name="signal")
         leak = keep.tile([P, 4], F32, name="leak")
         inv = keep.tile([P, 4], F32, name="inv")
@@ -49,12 +48,10 @@ def tile_downlink_leakage_rate_s12_kernel(tc, a_words, a_scales, v_words, v_scal
         b_codes = keep.tile([P, PASSES, 512], U32, name="b_codes", align_bytes=64)
         b_scales = keep.tile([P, PASSES, 512], U8, name="b_scales", align_bytes=64)
         b_raw = []
-        b_grp = []
+        bg = keep.tile([P, PASSES, 512, 4], BF16, name="bg", align_bytes=64)
         for g in range(PASSES):
             br = keep.tile([P, 4, 512], BF16, name=f"br{g}", align_bytes=64)
-            bg = keep.tile([P, 512, 4], BF16, name=f"bg{g}", align_bytes=64)
             b_raw.append(br)
-            b_grp.append(bg)
         v_raw = []
         v_cod = []
         f_raw = []
@@ -91,8 +88,8 @@ def tile_downlink_leakage_rate_s12_kernel(tc, a_words, a_scales, v_words, v_scal
             z_cod.append(zc)
             z_scl.append(zs)
             f_raw.append([])
-            for r in range(4):
-                fr = rows.tile([P, 1024], BF16, name="fr", align_bytes=64)
+            for h in range(2):
+                fr = rows.tile([P, 2, 1024], BF16, name="fr", align_bytes=64)
                 f_raw[G].append(fr)
 
         v_view = v_words.rearrange("g p c -> p g c")
@@ -100,10 +97,17 @@ def tile_downlink_leakage_rate_s12_kernel(tc, a_words, a_scales, v_words, v_scal
         def load_v(G):
             nc.sync.dma_start(out=v_raw[G][:].bitcast(I32), in_=v_view[:, :, 1024 * G : 1024 * (G + 1)].bitcast(I32))
 
+        def load_scales(eng, raw, source, quadrants, lo, hi):
+            for Q in quadrants:
+                eng.dma_start(
+                    out=raw[32 * Q : 32 * Q + 4, :, lo:hi].bitcast(I32),
+                    in_=source[:, 4 * Q : 4 * Q + 4, lo:hi].rearrange("g r n -> r g n").bitcast(I32),
+                )
+
         def load_f(G):
-            for r in range(4):
-                n0 = 512 * G + 128 * r
-                nc.sync.dma_start(out=f_raw[G][r][:], in_=f[n0 : n0 + 128, :])
+            for h in range(2):
+                n0 = 512 * G + 256 * h
+                nc.sync.dma_start(out=f_raw[G][h][:], in_=f[n0 : n0 + 256, :].rearrange("(r p) k -> p r k", p=P))
 
         def load_b(g):
             nc.sync.dma_start(out=b_raw[g][:], in_=b[512 * g : 512 * (g + 1), :].rearrange("(p j) w -> p j w", j=4))
@@ -122,19 +126,25 @@ def tile_downlink_leakage_rate_s12_kernel(tc, a_words, a_scales, v_words, v_scal
             nc.vector.tensor_copy(out=dst[:, :, lo:hi, :], in_=src[:, :, lo:hi, :])
 
         def interleave_b(g):
-            nc.vector.tensor_copy(out=b_grp[g][:], in_=b_raw[g][:].rearrange("p j w -> p w j"))
+            nc.vector.tensor_copy(
+                out=bg[:, g].rearrange("p (c i) j -> p c j i", i=4), in_=b_raw[g][:].rearrange("p j (c i) -> p c j i", i=4)
+            )
 
         def quant(codes, scales, grouped):
             nc.vector.quantize_mx(out=codes.bitcast(FP8X4), scales=scales, in_=grouped)
 
-        def quant_b(g):
-            quant(b_codes[:, g, :], b_scales[:, g, :], b_grp[g][:].rearrange("p w j -> p (w j)"))
-
-        def quant_f(G, g):
+        def quant_b():
             quant(
-                f_cod[G][:, g].rearrange("p t m -> p (t m)"),
-                f_scl[G][:, g].rearrange("p t m -> p (t m)"),
-                f_grp[G][:, g].rearrange("p t m j -> p (t m j)"),
+                b_codes[:].rearrange("p g w -> p (g w)"),
+                b_scales[:].rearrange("p g w -> p (g w)"),
+                bg[:].rearrange("p g w j -> p (g w j)"),
+            )
+
+        def quant_f(G):
+            quant(
+                f_cod[G][:].rearrange("p g t m -> p (g t m)"),
+                f_scl[G][:].rearrange("p g t m -> p (g t m)"),
+                f_grp[G][:].rearrange("p g t m j -> p (g t m j)"),
             )
 
         def quant_cols(cod, scl, grp, lo, hi):
@@ -146,23 +156,22 @@ def tile_downlink_leakage_rate_s12_kernel(tc, a_words, a_scales, v_words, v_scal
             else:
                 nc.scalar.copy(out, in_)
 
-        f_even_odd = {}
+        f_sorted = {}
 
-        def sort_f(G, r):
-            fe = rows.tile([P, PASSES, 2, P], F32, name="fe", bufs=12, align_bytes=64)
-            f_even_odd[G, r] = fe
-            nc.vector.tensor_copy(out=fe[:], in_=f_raw[G][r][:].bitcast(F32).rearrange("p (g x u) -> p g u x", g=PASSES, u=2))
+        def sort_f(G, h):
+            fe = rows.tile([P, 2, PASSES, 2, P], F32, name="fe", bufs=6, align_bytes=64)
+            f_sorted[G, h] = fe
+            nc.vector.tensor_copy(
+                out=fe[:].rearrange("p r g u x -> p (r g) u x"),
+                in_=f_raw[G][h][:].rearrange("p r k -> p (r k)").bitcast(F32).rearrange("p (q x u) -> p q u x", x=P, u=2),
+            )
 
         def turn_f(G, r, on_vector):
             bank = psum.tile([P, 2, PASSES, P], F32, name="bank")
-            words = f_raw[G][r][:].bitcast(F32)
+            words = f_sorted[G, r // 2]
             for g in range(PASSES):
                 for u in range(2):
-                    if (G, r) in f_even_odd:
-                        src = f_even_odd[G, r][:, g, u, :]
-                    else:
-                        src = words[:, 256 * g + u : 256 * (g + 1) : 2]
-                    nc.tensor.transpose(bank[:, u, g, :], src, perm[:].rearrange("p t b i -> p (t b i)"))
+                    nc.tensor.transpose(bank[:, u, g, :], words[:, r % 2, g, u, :], perm[:].rearrange("p t b i -> p (t b i)"))
             dst = f_grp[G][:].rearrange("p g t m j -> p (g t) (m j)").bitcast(F32)
             copy(
                 on_vector,
@@ -241,32 +250,21 @@ def tile_downlink_leakage_rate_s12_kernel(tc, a_words, a_scales, v_words, v_scal
 
         e_rows = {}
         diag = {}
-        off = {}
 
         def finish_tiles(m):
             dg = per.tile([P, P], F32, name="dg")
-            of = per.tile([P, P], F32, name="of")
             es = per.tile([P, 512], F32, name="es")
             diag[m] = dg
-            off[m] = of
             e_rows[m] = es
 
         def store_rows(m):
             nc.vector.tensor_copy(out=e_rows[m][:], in_=e_banks[m][:])
             nc.sync.dma_start(out=out_1[128 * m : 128 * (m + 1), :], in_=e_rows[m][:])
 
-        def split_diag(m, eng, src):
-            lo, hi = 128 * m, 128 * (m + 1)
-            eng.tensor_tensor(out=diag[m][:], in0=src[:, lo:hi], in1=ident[:], op=ALU.mult)
-            eng.tensor_tensor(out=off[m][:], in0=src[:, lo:hi], in1=diag[m][:], op=ALU.subtract)
-
-        def square_rest(m, src):
-            lo, hi = 128 * m, 128 * (m + 1)
+        def square_sum(src, total):
             sq = per.tile([P, 512], F32, name="sq")
-            if lo > 0:
-                nc.scalar.activation(sq[:, 0:lo], src[:, 0:lo], ACT.Square, accum_out=part_a[:, m : m + 1])
-            if hi < 512:
-                nc.scalar.activation(sq[:, hi:512], src[:, hi:512], ACT.Square, accum_out=part_b[:, m : m + 1])
+            width = src.shape[1]
+            nc.scalar.activation(sq[:, 0:width], src, ACT.Square, accum_out=total)
 
         def signal_power(m):
             junk = per.tile([P, P], F32, name="junk")
@@ -274,11 +272,8 @@ def tile_downlink_leakage_rate_s12_kernel(tc, a_words, a_scales, v_words, v_scal
                 out=junk[:], in0=diag[m][:], scalar=1.0, in1=diag[m][:], op0=ALU.mult, op1=ALU.mult, accum_out=signal[:, m : m + 1]
             )
 
-        def square_off(m):
-            nc.scalar.activation(off[m][:], off[m][:], ACT.Square, accum_out=part_off[:, m : m + 1])
-
         def log_rate(m):
-            nc.scalar.activation(rate[:, m : m + 1], inv[:, m : m + 1], ACT.Ln, bias=1.0, scale=signal[:, m : m + 1])
+            nc.scalar.activation(rate[:, m : m + 1], inv[:, m : m + 1], ACT.Ln, bias=0.0, scale=total[:, m : m + 1])
 
         nc.gpsimd.memset(asc[:].rearrange("p g c -> p (g c)").bitcast(I32), 0)
         nc.vector.memset(vs_raw[:].rearrange("p g c -> p (g c)").bitcast(I32), 0)
@@ -287,30 +282,22 @@ def tile_downlink_leakage_rate_s12_kernel(tc, a_words, a_scales, v_words, v_scal
         nc.scalar.activation(ln_warm[:], ln_warm[:], ACT.Ln)
         nc.sync.dma_start(out=aw[:].bitcast(I32), in_=a_words.rearrange("g p c -> p g c").bitcast(I32))
         load_v(0)
-        for Q in range(4):
-            nc.sync.dma_start(
-                out=vs_raw[32 * Q : 32 * Q + 4, :, :].bitcast(I32),
-                in_=v_scales[:, 4 * Q : 4 * Q + 4, :].rearrange("g r n -> r g n").bitcast(I32),
-            )
-        for Q in range(4):
-            nc.sync.dma_start(
-                out=asc[32 * Q : 32 * Q + 4, :, :].bitcast(I32),
-                in_=a_scales[:, 4 * Q : 4 * Q + 4, :].rearrange("g r n -> r g n").bitcast(I32),
-            )
+        load_scales(nc.sync, asc, a_scales, (0, 1), 0, 512)
+        load_scales(nc.gpsimd, asc, a_scales, (2, 3), 0, 512)
+        load_scales(nc.sync, vs_raw, v_scales, range(4), 0, 512)
+        load_scales(nc.sync, vs_raw, v_scales, range(4), 512, 2048)
         load_v(1)
+        load_f(0)
         load_b(0)
         load_v(2)
         load_b(1)
-        load_f(0)
-        load_v(3)
         load_f(1)
         load_f(2)
         load_f(3)
+        load_v(3)
 
         make_identity(nc, ident[:])
         nc.gpsimd.memset(rate[:], 0.0)
-        nc.gpsimd.memset(part_a[:], 0.0)
-        nc.gpsimd.memset(part_b[:], 0.0)
         warm_bank = psum.tile([P, 512], F32, name="bank")
         for i in range(WARM):
             nc.tensor.matmul(out=warm_bank[:], lhsT=zero[:, 0:128], rhs=zero[:], start=True, stop=True)
@@ -318,108 +305,89 @@ def tile_downlink_leakage_rate_s12_kernel(tc, a_words, a_scales, v_words, v_scal
         permute_v(0)
         permute_v_scales(0, 0, 16)
         permute_v_scales(1, 0, 16)
+        nc.vector.tensor_copy(out=perm[:], in_=ident[:].rearrange("p (b t i) -> p t b i", b=4, t=4))
         for n in range(4):
             channel(0, n, False)
         permute_v(1)
         permute_v_scales(0, 16, 64)
         permute_v_scales(1, 16, 64)
-        nc.vector.tensor_copy(out=perm[:], in_=ident[:].rearrange("p (b t i) -> p t b i", b=4, t=4))
         for n in range(4):
             channel(1, n, False)
+        for h in range(2):
+            sort_f(0, h)
         interleave_b(0)
         permute_v(2)
-        interleave_b(1)
-        for n in range(4):
-            channel(2, n, False)
-        quant_b(0)
-        quant_b(1)
-        for r in range(4):
-            sort_f(0, r)
-        permute_v(3)
-        for r in range(4):
-            turn_f(0, r, False)
         quant_h(0)
         for r in range(4):
-            sort_f(1, r)
+            turn_f(0, r, False)
+        interleave_b(1)
+        quant_b()
+        for h in range(2):
+            sort_f(1, h)
         for n in range(4):
-            channel(3, n, False)
-        for r in range(4):
-            sort_f(2, r)
-        quant_f(0, 0)
-        quant_f(0, 1)
-        for r in range(2):
-            sort_f(3, r)
+            channel(2, n, False)
+        quant_f(0)
         for r in range(4):
             turn_f(1, r, r % 2 == 1)
-        for r in range(2, 4):
-            sort_f(3, r)
-        for r in range(4):
-            turn_f(2, r, r % 2 == 1)
-        quant_f(1, 0)
-        quant_f(1, 1)
-        for r in range(4):
-            turn_f(3, r, r % 2 == 1)
-        quant_f(2, 0)
-        quant_f(2, 1)
+        for h in range(2):
+            sort_f(2, h)
         for n in range(4):
             precode(0, n, False)
-        quant_f(3, 0)
-        quant_f(3, 1)
+        quant_f(1)
+        for h in range(2):
+            sort_f(3, h)
+        for r in range(4):
+            turn_f(2, r, r % 2 == 1)
+        for r in range(4):
+            turn_f(3, r, r % 2 == 1)
+        quant_f(2)
+        permute_v(3)
+        for n in range(4):
+            precode(1, n, False)
+        quant_f(3)
         quant_h(1)
         quant_h(2)
         for n in range(4):
-            precode(1, n, n == 3)
-        quant_z(0, 0, 512)
-        quant_h(3)
-        for n in range(4):
             precode(2, n, n == 3)
+        quant_z(0, 0, 512)
         quant_z(1, 0, 512)
         for n in range(4):
             precode(3, n, n % 2 == 1)
-            if n == 1:
-                quant_z(2, 0, 512)
+        quant_z(2, 0, 512)
+        quant_z(3, 0, 512)
+        for n in range(4):
+            channel(3, n, n == 2)
+        quant_cols(h_cod[3], h_scl[3], h_grp[3], 0, 256)
+        quant_cols(h_cod[3], h_scl[3], h_grp[3], 256, 512)
         for m in range(4):
             finish_tiles(m)
-        for m in range(2):
-            for G in range(3):
+        for m in range(3):
+            for G in range(4):
                 effective(m, G)
-        quant_z(3, 0, 256)
-        quant_z(3, 256, 384)
-        quant_z(3, 384, 512)
-        effective(0, 3)
-        effective(1, 3)
-        for G in range(4):
-            effective(2, G)
         for half in (1, 0):
             for G in range(4):
                 effective_half(half, G)
+        hi_bank, lo_bank = e_halves[1], e_halves[0]
         for m in range(3):
+            square_sum(e_banks[m][:], total[:, m : m + 1])
             store_rows(m)
-            split_diag(m, nc.gpsimd, e_rows[m])
-            square_rest(m, e_rows[m])
+            nc.gpsimd.tensor_tensor(out=diag[m][:], in0=e_rows[m][:, 128 * m : 128 * (m + 1)], in1=ident[:], op=ALU.mult)
             if m > 0:
                 signal_power(m - 1)
-                square_off(m - 1)
-        hi_bank, lo_bank = e_halves[1], e_halves[0]
-        nc.vector.tensor_tensor(out=diag[3][:], in0=hi_bank[:, 128:256], in1=ident[:], op=ALU.mult)
-        signal_power(2)
-        nc.vector.tensor_tensor(out=off[3][:], in0=hi_bank[:, 128:256], in1=diag[3][:], op=ALU.subtract)
-        square_off(2)
-        sq3 = per.tile([P, 512], F32, name="sq")
-        nc.scalar.activation(sq3[:, 256:384], hi_bank[:, 0:128], ACT.Square, accum_out=part_b[:, 3:4])
-        nc.vector.tensor_copy(out=e_rows[3][:, 256:512], in_=hi_bank[:])
+        square_sum(hi_bank[:], half_sum[:, 1:2])
+        nc.scalar.copy(e_rows[3][:, 256:512], hi_bank[:])
         nc.sync.dma_start(out=out_1[384:512, 256:512], in_=e_rows[3][:, 256:512])
-        nc.scalar.activation(diag[3][:], diag[3][:], ACT.Square, accum_out=signal[:, 3:4])
-        square_off(3)
-        nc.scalar.activation(sq3[:, 0:256], lo_bank[:], ACT.Square, accum_out=part_a[:, 3:4])
-        nc.gpsimd.tensor_tensor(out=leak[:, 0:3], in0=part_a[:, 0:3], in1=part_b[:, 0:3], op=ALU.add)
-        nc.gpsimd.tensor_tensor(out=leak[:, 0:3], in0=leak[:, 0:3], in1=part_off[:, 0:3], op=ALU.add)
-        nc.vector.reciprocal(inv[:, 0:3], leak[:, 0:3])
+        nc.vector.tensor_tensor(out=diag[3][:], in0=e_rows[3][:, 384:512], in1=ident[:], op=ALU.mult)
+        signal_power(2)
+        nc.vector.tensor_tensor(out=leak[:, 0:3], in0=total[:, 0:3], in1=signal[:, 0:3], op=ALU.subtract)
+        square_sum(lo_bank[:], half_sum[:, 0:1])
+        square_sum(diag[3][:], signal[:, 3:4])
         nc.vector.scalar_tensor_tensor(
-            out=leak[:, 3:4], in0=part_a[:, 3:4], scalar=part_b[:, 3:4], in1=part_off[:, 3:4], op0=ALU.add, op1=ALU.add
+            out=leak[:, 3:4], in0=half_sum[:, 0:1], scalar=half_sum[:, 1:2], in1=signal[:, 3:4], op0=ALU.add, op1=ALU.subtract
         )
-        nc.vector.reciprocal(inv[:, 3:4], leak[:, 3:4])
-        nc.vector.tensor_copy(out=e_rows[3][:, 0:256], in_=lo_bank[:])
+        nc.vector.tensor_tensor(out=total[:, 3:4], in0=half_sum[:, 0:1], in1=half_sum[:, 1:2], op=ALU.add)
+        nc.vector.reciprocal(inv[:], leak[:])
+        nc.scalar.copy(e_rows[3][:, 0:256], lo_bank[:])
         nc.sync.dma_start(out=out_1[384:512, 0:256], in_=e_rows[3][:, 0:256])
         for m in range(4):
             log_rate(m)

from contextlib import ExitStack

import concourse.mybir as mybir
from concourse.masks import make_identity

F32 = mybir.dt.float32
BF16 = mybir.dt.bfloat16
I32 = mybir.dt.int32
U32 = mybir.dt.uint32
U8 = mybir.dt.uint8
FP8X4 = mybir.dt.float8_e4m3fn_x4
FP4X4 = mybir.dt.float4_e2m1fn_x4
ALU = mybir.AluOpType
ACT = mybir.ActivationFunctionType

P = 128
USERS, PATHS, ANT = 512, 1024, 2048
PASSES = 2
GROUPS = 4
FLOPS = 2 * USERS * PATHS * ANT * 2 + 2 * USERS * USERS * ANT
WARM = 13


def tile_downlink_leakage_rate_s12_kernel(tc, a_words, a_scales, v_words, v_scales, f, b, out_0, out_1):
    nc = tc.nc
    with ExitStack() as ctx:
        keep = ctx.enter_context(tc.tile_pool(name="keep", bufs=1))
        per = ctx.enter_context(tc.tile_pool(name="per", bufs=4))
        rows = ctx.enter_context(tc.tile_pool(name="rows", bufs=8))
        psum = ctx.enter_context(tc.psum_pool(name="psum", bufs=8))
        ctx.enter_context(tc.manual_schedule())

        aw = keep.tile([P, PASSES, 1024], U8, name="aw", align_bytes=64)
        asc = keep.tile([P, PASSES, 512], U8, name="asc", align_bytes=64)
        vs_raw = keep.tile([P, PASSES, 2048], U8, name="vs_raw", align_bytes=64)
        vs = keep.tile([P, PASSES, 4, 512], U8, name="vs", align_bytes=64)
        zero = keep.tile([P, 512], BF16, name="zero")
        ident = keep.tile([P, P], F32, name="ident")
        perm = keep.tile([P, 4, 4, 8], F32, name="perm")
        rate = keep.tile([P, P], F32, name="rate")
        ln_warm = keep.tile([P, 1], F32, name="ln_warm")
        total = keep.tile([P, 4], F32, name="total")
        half_sum = keep.tile([P, 2], F32, name="half_sum")
        signal = keep.tile([P, 4], F32, name="signal")
        leak = keep.tile([P, 4], F32, name="leak")
        inv = keep.tile([P, 4], F32, name="inv")
        rate_rows = keep.tile([4, P], F32, name="rate_rows")
        b_codes = keep.tile([P, PASSES, 512], U32, name="b_codes", align_bytes=64)
        b_scales = keep.tile([P, PASSES, 512], U8, name="b_scales", align_bytes=64)
        b_raw = []
        bg = keep.tile([P, PASSES, 512, 4], BF16, name="bg", align_bytes=64)
        for g in range(PASSES):
            br = keep.tile([P, 4, 512], BF16, name=f"br{g}", align_bytes=64)
            b_raw.append(br)
        v_raw = []
        v_cod = []
        f_raw = []
        f_grp = []
        f_cod = []
        f_scl = []
        h_grp = []
        h_cod = []
        h_scl = []
        z_grp = []
        z_cod = []
        z_scl = []
        for G in range(GROUPS):
            vr = per.tile([P, PASSES, 1024], U8, name="vr", align_bytes=64)
            vc = per.tile([P, 4, PASSES, 256], U8, name="vc", align_bytes=64)
            fg = per.tile([P, PASSES, 4, P, 4], BF16, name="fg", align_bytes=64)
            fc = per.tile([P, PASSES, 4, P], U32, name="fc", align_bytes=64)
            fs = per.tile([P, PASSES, 4, P], U8, name="fs", align_bytes=64)
            hg = per.tile([P, 512, 4], BF16, name="hg", align_bytes=64)
            hc = per.tile([P, 512], U32, name="hc", align_bytes=64)
            hs = per.tile([P, 512], U8, name="hs", align_bytes=64)
            zg = per.tile([P, 512, 4], BF16, name="zg", align_bytes=64)
            zc = per.tile([P, 512], U32, name="zc", align_bytes=64)
            zs = per.tile([P, 512], U8, name="zs", align_bytes=64)
            v_raw.append(vr)
            v_cod.append(vc)
            f_grp.append(fg)
            f_cod.append(fc)
            f_scl.append(fs)
            h_grp.append(hg)
            h_cod.append(hc)
            h_scl.append(hs)
            z_grp.append(zg)
            z_cod.append(zc)
            z_scl.append(zs)
            f_raw.append([])
            for h in range(2):
                fr = rows.tile([P, 2, 1024], BF16, name="fr", align_bytes=64)
                f_raw[G].append(fr)

        v_view = v_words.rearrange("g p c -> p g c")

        def load_v(G):
            nc.sync.dma_start(out=v_raw[G][:].bitcast(I32), in_=v_view[:, :, 1024 * G : 1024 * (G + 1)].bitcast(I32))

        def load_scales(eng, raw, source, quadrants, lo, hi):
            for Q in quadrants:
                eng.dma_start(
                    out=raw[32 * Q : 32 * Q + 4, :, lo:hi].bitcast(I32),
                    in_=source[:, 4 * Q : 4 * Q + 4, lo:hi].rearrange("g r n -> r g n").bitcast(I32),
                )

        def load_f(G):
            for h in range(2):
                n0 = 512 * G + 256 * h
                nc.sync.dma_start(out=f_raw[G][h][:], in_=f[n0 : n0 + 256, :].rearrange("(r p) k -> p r k", p=P))

        def load_b(g):
            nc.sync.dma_start(out=b_raw[g][:], in_=b[512 * g : 512 * (g + 1), :].rearrange("(p j) w -> p j w", j=4))

        def permute_v(G):
            src = v_raw[G][:].rearrange("p g c -> p (g c)").bitcast(I32)
            dst = v_cod[G][:].rearrange("p t g c -> p (t g c)").bitcast(I32)
            nc.vector.tensor_copy(
                out=dst.rearrange("p (t b w) -> p t b w", t=4, w=4),
                in_=src.rearrange("p (b t w) -> p t b w", t=4, w=4),
            )

        def permute_v_scales(g, lo, hi):
            src = vs_raw[:, g, :].bitcast(I32).rearrange("p (b t w) -> p t b w", t=4, w=2)
            dst = vs[:, g, :, :].rearrange("p t c -> p (t c)").bitcast(I32).rearrange("p (t b w) -> p t b w", t=4, w=2)
            nc.vector.tensor_copy(out=dst[:, :, lo:hi, :], in_=src[:, :, lo:hi, :])

        def interleave_b(g):
            nc.vector.tensor_copy(
                out=bg[:, g].rearrange("p (c i) j -> p c j i", i=4), in_=b_raw[g][:].rearrange("p j (c i) -> p c j i", i=4)
            )

        def quant(codes, scales, grouped):
            nc.vector.quantize_mx(out=codes.bitcast(FP8X4), scales=scales, in_=grouped)

        def quant_b():
            quant(
                b_codes[:].rearrange("p g w -> p (g w)"),
                b_scales[:].rearrange("p g w -> p (g w)"),
                bg[:].rearrange("p g w j -> p (g w j)"),
            )

        def quant_f(G):
            quant(
                f_cod[G][:].rearrange("p g t m -> p (g t m)"),
                f_scl[G][:].rearrange("p g t m -> p (g t m)"),
                f_grp[G][:].rearrange("p g t m j -> p (g t m j)"),
            )

        def quant_cols(cod, scl, grp, lo, hi):
            quant(cod[:, lo:hi], scl[:, lo:hi], grp[:, lo:hi, :].rearrange("p n j -> p (n j)"))

        def copy(on_vector, out, in_):
            if on_vector:
                nc.vector.tensor_copy(out=out, in_=in_)
            else:
                nc.scalar.copy(out, in_)

        f_sorted = {}

        def sort_f(G, h):
            fe = rows.tile([P, 2, PASSES, 2, P], F32, name="fe", bufs=6, align_bytes=64)
            f_sorted[G, h] = fe
            nc.vector.tensor_copy(
                out=fe[:].rearrange("p r g u x -> p (r g) u x"),
                in_=f_raw[G][h][:].rearrange("p r k -> p (r k)").bitcast(F32).rearrange("p (q x u) -> p q u x", x=P, u=2),
            )

        def turn_f(G, r, on_vector):
            bank = psum.tile([P, 2, PASSES, P], F32, name="bank")
            words = f_sorted[G, r // 2]
            for g in range(PASSES):
                for u in range(2):
                    nc.tensor.transpose(bank[:, u, g, :], words[:, r % 2, g, u, :], perm[:].rearrange("p t b i -> p (t b i)"))
            dst = f_grp[G][:].rearrange("p g t m j -> p (g t) (m j)").bitcast(F32)
            copy(
                on_vector,
                dst[:, :, 64 * r : 64 * (r + 1)].rearrange("p q (c u) -> p q c u", u=2),
                bank[:].rearrange("p u g c -> p u (g c)").rearrange("p u (q c) -> p q c u", c=32),
            )

        def channel(G, n, on_vector):
            bank = psum.tile([P, 4, P], F32, name="bank")
            for t in range(4):
                for g in range(PASSES):
                    nc.tensor.matmul_mx(
                        out=bank[:, t, :],
                        lhsT=v_cod[G][:, t, g, :].bitcast(FP4X4),
                        lhsT_scale=vs[:, g, t, 128 * G : 128 * (G + 1)],
                        rhs=aw[:, g, 256 * n : 256 * (n + 1)].bitcast(FP4X4),
                        rhs_scale=asc[:, g, 128 * n : 128 * (n + 1)],
                        start=(g == 0),
                        stop=(g == PASSES - 1),
                    )
            copy(on_vector, h_grp[G][:, 128 * n : 128 * (n + 1), :], bank[:].rearrange("p t c -> p c t"))

        def precode(G, n, on_vector):
            bank = psum.tile([P, 4, P], F32, name="bank")
            for t in range(4):
                for g in range(PASSES):
                    nc.tensor.matmul_mx(
                        out=bank[:, t, :],
                        lhsT=f_cod[G][:, g, t, :].bitcast(FP8X4),
                        lhsT_scale=f_scl[G][:, g, t, :],
                        rhs=b_codes[:, g, 128 * n : 128 * (n + 1)].bitcast(FP8X4),
                        rhs_scale=b_scales[:, g, 128 * n : 128 * (n + 1)],
                        start=(g == 0),
                        stop=(g == PASSES - 1),
                    )
            copy(on_vector, z_grp[G][:, 128 * n : 128 * (n + 1), :], bank[:].rearrange("p t c -> p c t"))

        def quant_h(G):
            quant_cols(h_cod[G], h_scl[G], h_grp[G], 0, 512)

        def quant_z(G, lo, hi):
            quant_cols(z_cod[G], z_scl[G], z_grp[G], lo, hi)

        e_banks = {}

        def effective(m, G):
            if G == 0:
                eb = psum.tile([P, 512], F32, name="bank")
                e_banks[m] = eb
            nc.tensor.matmul_mx(
                out=e_banks[m][:],
                lhsT=h_cod[G][:, 128 * m : 128 * (m + 1)].bitcast(FP8X4),
                lhsT_scale=h_scl[G][:, 128 * m : 128 * (m + 1)],
                rhs=z_cod[G][:].bitcast(FP8X4),
                rhs_scale=z_scl[G][:],
                start=(G == 0),
                stop=(G == GROUPS - 1),
            )

        e_halves = {}

        def effective_half(half, G):
            if G == 0:
                eb = psum.tile([P, 256], F32, name="bank")
                e_halves[half] = eb
            cols = slice(256 * half, 256 * (half + 1))
            nc.tensor.matmul_mx(
                out=e_halves[half][:],
                lhsT=h_cod[G][:, 384:512].bitcast(FP8X4),
                lhsT_scale=h_scl[G][:, 384:512],
                rhs=z_cod[G][:, cols].bitcast(FP8X4),
                rhs_scale=z_scl[G][:, cols],
                start=(G == 0),
                stop=(G == GROUPS - 1),
            )

        e_rows = {}
        diag = {}

        def finish_tiles(m):
            dg = per.tile([P, P], F32, name="dg")
            es = per.tile([P, 512], F32, name="es")
            diag[m] = dg
            e_rows[m] = es

        def store_rows(m):
            nc.vector.tensor_copy(out=e_rows[m][:], in_=e_banks[m][:])
            nc.sync.dma_start(out=out_1[128 * m : 128 * (m + 1), :], in_=e_rows[m][:])

        def square_sum(src, total):
            sq = per.tile([P, 512], F32, name="sq")
            width = src.shape[1]
            nc.scalar.activation(sq[:, 0:width], src, ACT.Square, accum_out=total)

        def signal_power(m):
            junk = per.tile([P, P], F32, name="junk")
            nc.vector.scalar_tensor_tensor(
                out=junk[:], in0=diag[m][:], scalar=1.0, in1=diag[m][:], op0=ALU.mult, op1=ALU.mult, accum_out=signal[:, m : m + 1]
            )

        def log_rate(m):
            nc.scalar.activation(rate[:, m : m + 1], inv[:, m : m + 1], ACT.Ln, bias=0.0, scale=total[:, m : m + 1])

        nc.gpsimd.memset(asc[:].rearrange("p g c -> p (g c)").bitcast(I32), 0)
        nc.vector.memset(vs_raw[:].rearrange("p g c -> p (g c)").bitcast(I32), 0)
        nc.vector.memset(zero[:], 0.0)
        nc.vector.memset(ln_warm[:], 1.0)
        nc.scalar.activation(ln_warm[:], ln_warm[:], ACT.Ln)
        nc.sync.dma_start(out=aw[:].bitcast(I32), in_=a_words.rearrange("g p c -> p g c").bitcast(I32))
        load_v(0)
        load_scales(nc.sync, asc, a_scales, (0, 1), 0, 512)
        load_scales(nc.gpsimd, asc, a_scales, (2, 3), 0, 512)
        load_scales(nc.sync, vs_raw, v_scales, range(4), 0, 512)
        load_scales(nc.sync, vs_raw, v_scales, range(4), 512, 2048)
        load_v(1)
        load_f(0)
        load_b(0)
        load_v(2)
        load_b(1)
        load_f(1)
        load_f(2)
        load_f(3)
        load_v(3)

        make_identity(nc, ident[:])
        nc.gpsimd.memset(rate[:], 0.0)
        warm_bank = psum.tile([P, 512], F32, name="bank")
        for i in range(WARM):
            nc.tensor.matmul(out=warm_bank[:], lhsT=zero[:, 0:128], rhs=zero[:], start=True, stop=True)

        permute_v(0)
        permute_v_scales(0, 0, 16)
        permute_v_scales(1, 0, 16)
        nc.vector.tensor_copy(out=perm[:], in_=ident[:].rearrange("p (b t i) -> p t b i", b=4, t=4))
        for n in range(4):
            channel(0, n, False)
        permute_v(1)
        permute_v_scales(0, 16, 64)
        permute_v_scales(1, 16, 64)
        for n in range(4):
            channel(1, n, False)
        for h in range(2):
            sort_f(0, h)
        interleave_b(0)
        permute_v(2)
        quant_h(0)
        for r in range(4):
            turn_f(0, r, False)
        interleave_b(1)
        quant_b()
        for h in range(2):
            sort_f(1, h)
        for n in range(4):
            channel(2, n, False)
        quant_f(0)
        for r in range(4):
            turn_f(1, r, r % 2 == 1)
        for h in range(2):
            sort_f(2, h)
        for n in range(4):
            precode(0, n, False)
        quant_f(1)
        for h in range(2):
            sort_f(3, h)
        for r in range(4):
            turn_f(2, r, r % 2 == 1)
        for r in range(4):
            turn_f(3, r, r % 2 == 1)
        quant_f(2)
        permute_v(3)
        for n in range(4):
            precode(1, n, False)
        quant_f(3)
        quant_h(1)
        quant_h(2)
        for n in range(4):
            precode(2, n, n == 3)
        quant_z(0, 0, 512)
        quant_z(1, 0, 512)
        for n in range(4):
            precode(3, n, n % 2 == 1)
        quant_z(2, 0, 512)
        quant_z(3, 0, 512)
        for n in range(4):
            channel(3, n, n == 2)
        quant_cols(h_cod[3], h_scl[3], h_grp[3], 0, 256)
        quant_cols(h_cod[3], h_scl[3], h_grp[3], 256, 512)
        for m in range(4):
            finish_tiles(m)
        for m in range(3):
            for G in range(4):
                effective(m, G)
        for half in (1, 0):
            for G in range(4):
                effective_half(half, G)
        hi_bank, lo_bank = e_halves[1], e_halves[0]
        for m in range(3):
            square_sum(e_banks[m][:], total[:, m : m + 1])
            store_rows(m)
            nc.gpsimd.tensor_tensor(out=diag[m][:], in0=e_rows[m][:, 128 * m : 128 * (m + 1)], in1=ident[:], op=ALU.mult)
            if m > 0:
                signal_power(m - 1)
        square_sum(hi_bank[:], half_sum[:, 1:2])
        nc.scalar.copy(e_rows[3][:, 256:512], hi_bank[:])
        nc.sync.dma_start(out=out_1[384:512, 256:512], in_=e_rows[3][:, 256:512])
        nc.vector.tensor_tensor(out=diag[3][:], in0=e_rows[3][:, 384:512], in1=ident[:], op=ALU.mult)
        signal_power(2)
        nc.vector.tensor_tensor(out=leak[:, 0:3], in0=total[:, 0:3], in1=signal[:, 0:3], op=ALU.subtract)
        square_sum(lo_bank[:], half_sum[:, 0:1])
        square_sum(diag[3][:], signal[:, 3:4])
        nc.vector.scalar_tensor_tensor(
            out=leak[:, 3:4], in0=half_sum[:, 0:1], scalar=half_sum[:, 1:2], in1=signal[:, 3:4], op0=ALU.add, op1=ALU.subtract
        )
        nc.vector.tensor_tensor(out=total[:, 3:4], in0=half_sum[:, 0:1], in1=half_sum[:, 1:2], op=ALU.add)
        nc.vector.reciprocal(inv[:], leak[:])
        nc.scalar.copy(e_rows[3][:, 0:256], lo_bank[:])
        nc.sync.dma_start(out=out_1[384:512, 0:256], in_=e_rows[3][:, 0:256])
        for m in range(4):
            log_rate(m)

        last = psum.tile([P, 4, P], F32, name="bank")
        nc.tensor.transpose(last[:, 0, :], rate[:], ident[:])
        nc.vector.tensor_copy(out=rate_rows[:], in_=last[0:4, 0, :])
        nc.sync.dma_start(out=out_0.rearrange("(m p) -> m p", p=P), in_=rate_rows[:])
